import numpy as np
import ml_dtypes


def mxq(x, axis, fmt="e4m3"):
    dtype, down = {"e4m3": (ml_dtypes.float8_e4m3fn, 7), "e5m2": (ml_dtypes.float8_e5m2, 14)}[fmt]
    v = np.moveaxis(np.asarray(x, np.float32).astype(ml_dtypes.bfloat16).astype(np.float64), axis, -1)
    blocks = v.reshape(v.shape[:-1] + (-1, 32))
    amax = np.abs(blocks).max(-1, keepdims=True)
    byte = np.maximum(np.where(amax > 0, np.frexp(amax)[1] - 1 + 127, 0) - down, 1)
    scale = np.exp2(byte - 127.0)
    codes = (blocks / scale).astype(np.float32).astype(dtype).astype(np.float64)
    return np.moveaxis((codes * scale).reshape(v.shape), -1, axis)


WIDE = False


def mx_kscale(k, group=512):
    if not WIDE:
        return np.ones(k)
    levels = np.array([10, -10, 5, -5, 0])
    if group != 512:
        return np.exp2(np.random.permutation(np.resize(levels, k // group))).repeat(group)
    if k % 512:
        return np.exp2(np.random.permutation(np.resize(levels, k // 32))).repeat(32)
    a = np.empty((k // 512, 16))
    for p in range(k // 512):
        a[p, :8] = np.random.permutation(np.resize(levels, 8))
        for g in range(8):
            far = levels[np.abs(levels - a[p, g]) >= 10]
            a[p, g + 8] = far[np.random.randint(len(far))]
    return np.exp2(a.ravel()).repeat(32)


def f64(x):
    return np.asarray(x).astype(np.float64)


E2M1 = np.array([0.0, 0.5, 1.0, 1.5, 2.0, 3.0, 4.0, 6.0, -0.0, -0.5, -1.0, -1.5, -2.0, -3.0, -4.0, -6.0])


def pack_group(w):
    k, n = w.shape
    w = f64(np.asarray(w, np.float32).astype(ml_dtypes.bfloat16)).reshape(k // 32, 32, n)
    amax = np.abs(w).max(1)
    mant, ex = np.frexp(amax / 6.0)
    byte = np.clip(np.where(amax > 0, np.where(mant > 0.5, ex, ex - 1) + 127, 1), 1, 254)
    scaled = (w * np.exp2(127.0 - byte)[:, None, :]).reshape(k, n).astype(np.float32)
    c = np.ascontiguousarray(scaled.reshape(k // 4, 4, n).transpose(0, 2, 1)).astype(ml_dtypes.float4_e2m1fn).view(np.uint8) & 0xF
    return np.ascontiguousarray((c[..., 0::2] | (c[..., 1::2] << 4)).reshape(k // 4, 2 * n)), byte.astype(np.uint8)


def unpack_group(words, scales):
    p, n = words.shape[0], scales.shape[1]
    words = np.ascontiguousarray(words).reshape(p, n, 2)
    nib = np.empty((p, n, 4), np.uint8)
    nib[..., 0::2] = words & 0xF
    nib[..., 1::2] = words >> 4
    return E2M1[nib].transpose(0, 2, 1).reshape(4 * p, n) * np.repeat(np.exp2(scales.astype(np.float64) - 127.0), 32, axis=0)


G, D, M, O, N = 2, 256, 256, 256, 512


def setup_inputs():
    n = np.random.standard_normal
    s_d = mx_kscale(D, 0)
    s_o = mx_kscale(O, 0)
    w1_ = [pack_group(w) for w in n((G, D, M)) / np.sqrt(D) / s_d[:, None]]
    w2_ = [pack_group(w) for w in n((G, D, M)) / np.sqrt(D) / s_d[:, None]]
    wo_ = [pack_group(w) for w in n((G, O, M)) / np.sqrt(O) / s_o[:, None]]
    return {
        "x": (n((G, D, N)) * s_d[:, None]).astype(np.float32),
        "w1_words": np.stack([w[0] for w in w1_]),
        "w1_scales": np.stack([w[1] for w in w1_]),
        "w2_words": np.stack([w[0] for w in w2_]),
        "w2_scales": np.stack([w[1] for w in w2_]),
        "so": (np.random.uniform(0.3, 1.0, (G, M, 1))).astype(np.float32),
        "wo_words": np.stack([w[0] for w in wo_]),
        "wo_scales": np.stack([w[1] for w in wo_]),
        "dy": (n((G, O, N)) * s_o[:, None]).astype(np.float32),
        "old": (0.3 * n((G, M, N))).astype(np.float32),
    }


def reference(x, w1_words, w1_scales, w2_words, w2_scales, so, wo_words, wo_scales, dy, old):
    w1 = np.stack([unpack_group(w1_words[g], w1_scales[g]) for g in range(G)])
    xq = mxq(f64(x), 1, "e4m3")
    z1 = w1.transpose(0, 2, 1) @ xq
    w2 = np.stack([unpack_group(w2_words[g], w2_scales[g]) for g in range(G)])
    z2 = w2.transpose(0, 2, 1) @ xq
    nm = np.sqrt(np.square(z1) * np.square(z2) + f64(so))
    wo = np.stack([unpack_group(wo_words[g], wo_scales[g]) for g in range(G)])
    dyq = mxq(f64(dy), 1, "e4m3")
    c0 = wo.transpose(0, 2, 1) @ dyq
    dnm = c0 * z1 * z2 / np.square(nm) * (-1.0)
    dz1 = c0 / nm * z2 + dnm * 0.5 / np.sqrt(np.square(z1) * np.square(z2) + f64(so)) * np.square(z2) * z1 * 2.0
    y = dz1 + f64(old)
    return y

@@ -1,0 +1,175 @@
+from contextlib import ExitStack
+
+import concourse.mybir as mybir
+
+G, D, M, N = 2, 256, 256, 512
+FLOPS = 3 * 2 * G * D * M * N
+
+F32 = mybir.dt.float32
+BF16 = mybir.dt.bfloat16
+I32 = mybir.dt.int32
+U32 = mybir.dt.uint32
+U8 = mybir.dt.uint8
+FP8X4 = mybir.dt.float8_e4m3fn_x4
+FP4X4 = mybir.dt.float4_e2m1fn_x4
+ACT = mybir.ActivationFunctionType
+ALU = mybir.AluOpType
+
+P = 128
+PACK = 4
+ROWS = D // PACK
+HALVES = M // P
+TILES = [(g, h) for h in range(HALVES) for g in range(G)]
+UNIT = 256
+PER_TILE = N // UNIT
+UNITS = len(TILES) * PER_TILE
+X_VECTOR_COLS = 320
+DY_VECTOR_COLS = 416
+POOL_SUMS = 2
+
+
+def tile_rows_bagree_kernel(tc, x, w1_words, w1_scales, w2_words, w2_scales, so, wo_words, wo_scales, dy, old, out):
+    nc = tc.nc
+    with ExitStack() as ctx:
+        sb = ctx.enter_context(tc.tile_pool(name="sb", bufs=1))
+        ps = ctx.enter_context(tc.psum_pool(name="ps", bufs=1))
+        ctx.enter_context(tc.manual_schedule())
+
+        def words_tile(name):
+            return sb.tile([P, 2 * M], U8, name=name, align_bytes=64)
+
+        def plane_tile(name, width):
+            return sb.tile([P, width], U8, name=name, align_bytes=64)
+
+        def load_words(queue, tile, words):
+            queue.dma_start(out=tile[:].bitcast(I32), in_=words.rearrange("g p b -> (g p) b").bitcast(I32))
+
+        def load_scales(queue, tile, scales):
+            rows = scales.rearrange("g t m -> (g t) m").bitcast(I32)
+            for q in range(4):
+                queue.dma_start(out=tile[32 * q : 32 * q + 4, :].bitcast(I32), in_=rows[4 * q : 4 * q + 4, :])
+
+        def interleave(copy, packed, raw, cols):
+            copy(
+                out=packed.rearrange("p (c i) j -> p c j i", i=4),
+                in_=raw[:, :, cols].rearrange("p j (c i) -> p c j i", i=4),
+            )
+
+        def quantize(codes, plane, cols, packed):
+            nc.vector.quantize_mx(
+                out=codes[:, cols].bitcast(FP8X4), scales=plane[:, cols], in_=packed[:].rearrange("p n j -> p (n j)")
+            )
+
+        def product(bank, t, words, w_plane, codes, plane):
+            g, h = TILES[t]
+            rows = slice(ROWS * g, ROWS * (g + 1))
+            nc.tensor.matmul_mx(
+                out=bank[:],
+                lhsT=words[rows, 2 * P * h : 2 * P * (h + 1)].bitcast(FP4X4),
+                lhsT_scale=w_plane[rows, P * h : P * (h + 1)],
+                rhs=codes[rows, :].bitcast(FP8X4),
+                rhs_scale=plane[rows, :],
+                start=True,
+                stop=True,
+            )
+
+        w1, w2, wo = words_tile("w1"), words_tile("w2"), words_tile("wo")
+        s1, s2, s_o = plane_tile("s1", M), plane_tile("s2", M), plane_tile("s_o", M)
+        x_raw = sb.tile([P, PACK, N], F32, name="x_raw")
+        dy_raw = sb.tile([P, PACK, N], F32, name="dy_raw")
+        soft = sb.tile([P, G * HALVES, 8], F32, name="soft")
+        olds = [sb.tile([P, N], F32, name="old%d" % t) for t in range(len(TILES))]
+        results = [sb.tile([P, N], F32, name="result%d" % t) for t in range(len(TILES))]
+
+        nc.vector.memset(s2[:].bitcast(I32), 0)
+        nc.gpsimd.memset(s1[:].bitcast(I32), 0)
+        nc.vector.memset(s_o[:].bitcast(I32), 0)
+        nc.sync.dma_start(out=x_raw[:], in_=x.rearrange("g (p j) n -> (g p) j n", j=PACK))
+        nc.sync.dma_start(out=dy_raw[:], in_=dy.rearrange("g (p j) n -> (g p) j n", j=PACK))
+        load_words(nc.scalar, w2, w2_words)
+        load_words(nc.scalar, w1, w1_words)
+        load_scales(nc.scalar, s2, w2_scales)
+        load_scales(nc.gpsimd, s1, w1_scales)
+        load_words(nc.sync, wo, wo_words)
+        load_scales(nc.sync, s_o, wo_scales)
+        with nc.allow_non_contiguous_dma(reason="one softener a partition"):
+            nc.sync.dma_start(out=soft[:, :, 0:1], in_=so.rearrange("g (h p) o -> p (g h) o", p=P))
+        for t, (g, h) in enumerate(TILES):
+            nc.sync.dma_start(out=olds[t][:], in_=old[g, P * h : P * (h + 1), :])
+
+        half = N // 2
+        x_lo = sb.tile([P, half, PACK], BF16, name="x_lo", align_bytes=64)
+        x_hi = sb.tile([P, half, PACK], BF16, name="x_hi", align_bytes=64)
+        x_codes = sb.tile([P, N], U32, name="x_codes", align_bytes=64)
+        x_plane = plane_tile("x_plane", N)
+        interleave(nc.scalar.copy, x_hi[:, X_VECTOR_COLS - half :, :], x_raw, slice(X_VECTOR_COLS, N))
+        interleave(nc.vector.tensor_copy, x_lo[:], x_raw, slice(0, half))
+        interleave(nc.vector.tensor_copy, x_hi[:, : X_VECTOR_COLS - half, :], x_raw, slice(half, X_VECTOR_COLS))
+        quantize(x_codes, x_plane, slice(0, half), x_lo)
+        quantize(x_codes, x_plane, slice(half, N), x_hi)
+
+        z2_banks = [ps.tile([P, N], F32, name="z2_%d" % t) for t in range(len(TILES))]
+        z1_banks = [ps.tile([P, N], F32, name="z1_%d" % t) for t in range(len(TILES))]
+        for h in range(HALVES):
+            for t in range(G * h, G * (h + 1)):
+                product(z2_banks[t], t, w2, s2, x_codes, x_plane)
+            for t in range(G * h, G * (h + 1)):
+                product(z1_banks[t], t, w1, s1, x_codes, x_plane)
+
+        dy_packed = sb.tile([P, N, PACK], BF16, name="dy_packed", align_bytes=64)
+        dy_codes = sb.tile([P, N], U32, name="dy_codes", align_bytes=64)
+        dy_plane = plane_tile("dy_plane", N)
+        interleave(nc.scalar.copy, dy_packed[:, DY_VECTOR_COLS:, :], dy_raw, slice(DY_VECTOR_COLS, N))
+        interleave(nc.vector.tensor_copy, dy_packed[:, :DY_VECTOR_COLS, :], dy_raw, slice(0, DY_VECTOR_COLS))
+
+        z2_copies = [sb.tile([P, N], F32, name="z2_copy%d" % t) for t in range(len(TILES))]
+        stages = ("prod", "sq", "root", "inv", "left", "right", "grad")
+        val = {(k, u): sb.tile([P, UNIT], F32, name="%s%d" % (k, u)) for k in stages for u in range(UNITS)}
+
+        def place(u):
+            t = u // PER_TILE
+            g, h = TILES[t]
+            c = HALVES * g + h
+            return t, slice(UNIT * (u % PER_TILE), UNIT * (u % PER_TILE + 1)), soft[:, c, 0:1]
+
+        for step in range(-2, UNITS + 3):
+            u = step + 2
+            if u < UNITS:
+                t, cols = place(u)[:2]
+                if u % PER_TILE == 0:
+                    nc.scalar.copy(out=z2_copies[t][:], in_=z2_banks[t][:])
+                nc.vector.tensor_tensor(out=val["prod", u][:], in0=z1_banks[t][:, cols], in1=z2_copies[t][:, cols], op=ALU.mult)
+                if u == PER_TILE - 1:
+                    quantize(dy_codes, dy_plane, slice(0, N), dy_packed)
+                if u % PER_TILE == PER_TILE - 1:
+                    product(z1_banks[t], t, wo, s_o, dy_codes, dy_plane)
+            u = step
+            if 0 <= u < UNITS:
+                nc.scalar.activation(out=val["sq", u][:], in_=val["prod", u][:], func=ACT.Square)
+            u = step - 1
+            if 0 <= u < UNITS:
+                nc.scalar.activation(out=val["inv", u][:], in_=val["root", u][:], func=ACT.Square)
+            u = step
+            if 0 <= u < UNITS:
+                nc.scalar.activation(out=val["root", u][:], in_=val["sq", u][:], func=ACT.Abs_reciprocal_sqrt, bias=place(u)[2])
+            u = step - 1
+            if 0 <= u < UNITS:
+                t, cols, softener = place(u)
+                nc.vector.scalar_tensor_tensor(
+                    out=val["left", u][:], in0=z1_banks[t][:, cols], scalar=softener, in1=val["root", u][:], op0=ALU.mult, op1=ALU.mult
+                )
+                nc.vector.tensor_tensor(out=val["right", u][:], in0=z2_banks[t][:, cols], in1=val["inv", u][:], op=ALU.mult)
+            u = step - 2
+            if 0 <= u < UNITS:
+                engine = nc.gpsimd if u < UNITS - 1 else nc.vector
+                engine.tensor_tensor(out=val["grad", u][:], in0=val["left", u][:], in1=val["right", u][:], op=ALU.mult)
+            u = step - 3
+            if 0 <= u < UNITS:
+                t, cols = place(u)[:2]
+                g, h = TILES[t]
+                engine = nc.gpsimd if u < POOL_SUMS else nc.vector
+                engine.tensor_tensor(out=results[t][:, cols], in0=val["grad", u][:], in1=olds[t][:, cols], op=ALU.add)
+                if t == len(TILES) - 1:
+                    nc.sync.dma_start(out=out[g, P * h : P * (h + 1), cols], in_=results[t][:, cols])
+                elif u % PER_TILE == PER_TILE - 1:
+                    nc.sync.dma_start(out=out[g, P * h : P * (h + 1), :], in_=results[t][:])

@@ -83,12 +83,15 @@ def tile_rows_bagree_kernel(tc, x, w1_words, w1_scales, w2_words, w2_scales, so,
 
         nc.vector.memset(s2[:].bitcast(I32), 0)
         nc.gpsimd.memset(s1[:].bitcast(I32), 0)
+        warm = sb.tile([P, 16], F32, name="warm")
+        nc.vector.memset(warm[:, 0:1], 1.0)
         nc.vector.memset(s_o[:].bitcast(I32), 0)
         nc.sync.dma_start(out=x_raw[:], in_=x.rearrange("g (p j) n -> (g p) j n", j=PACK))
         nc.sync.dma_start(out=dy_raw[:], in_=dy.rearrange("g (p j) n -> (g p) j n", j=PACK))
         load_words(nc.scalar, w2, w2_words)
         load_words(nc.scalar, w1, w1_words)
         load_scales(nc.scalar, s2, w2_scales)
+        nc.scalar.activation(out=warm[:, 8:9], in_=warm[:, 0:1], func=ACT.Abs_reciprocal_sqrt)
         load_scales(nc.gpsimd, s1, w1_scales)
         load_words(nc.sync, wo, wo_words)
         load_scales(nc.sync, s_o, wo_scales)

@@ -25,7 +25,8 @@ PER_TILE = N // UNIT
 UNITS = len(TILES) * PER_TILE
 X_VECTOR_COLS = 320
 DY_VECTOR_COLS = 416
-POOL_SUMS = 2
+POOL_SQUARES = 2
+LEAD = 4
 
 
 def tile_rows_bagree_kernel(tc, x, w1_words, w1_scales, w2_words, w2_scales, so, wo_words, wo_scales, dy, old, out):
@@ -87,10 +88,10 @@ def tile_rows_bagree_kernel(tc, x, w1_words, w1_scales, w2_words, w2_scales, so,
         nc.vector.memset(warm[:, 0:1], 1.0)
         nc.vector.memset(s_o[:].bitcast(I32), 0)
         nc.sync.dma_start(out=x_raw[:], in_=x.rearrange("g (p j) n -> (g p) j n", j=PACK))
+        load_words(nc.sync, w2, w2_words)
+        load_words(nc.sync, w1, w1_words)
+        load_scales(nc.sync, s2, w2_scales)
         nc.sync.dma_start(out=dy_raw[:], in_=dy.rearrange("g (p j) n -> (g p) j n", j=PACK))
-        load_words(nc.scalar, w2, w2_words)
-        load_words(nc.scalar, w1, w1_words)
-        load_scales(nc.scalar, s2, w2_scales)
         nc.scalar.activation(out=warm[:, 8:9], in_=warm[:, 0:1], func=ACT.Abs_reciprocal_sqrt)
         load_scales(nc.gpsimd, s1, w1_scales)
         load_words(nc.sync, wo, wo_words)
@@ -135,43 +136,44 @@ def tile_rows_bagree_kernel(tc, x, w1_words, w1_scales, w2_words, w2_scales, so,
             c = HALVES * g + h
             return t, slice(UNIT * (u % PER_TILE), UNIT * (u % PER_TILE + 1)), soft[:, c, 0:1]
 
-        for step in range(-2, UNITS + 3):
-            u = step + 2
+        for t in range(len(TILES)):
+            nc.scalar.copy(out=z2_copies[t][:], in_=z2_banks[t][:])
+
+        for step in range(-LEAD, UNITS + 3):
+            u = step + LEAD
+            if u == 1:
+                quantize(dy_codes, dy_plane, slice(0, N), dy_packed)
             if u < UNITS:
                 t, cols = place(u)[:2]
-                if u % PER_TILE == 0:
-                    nc.scalar.copy(out=z2_copies[t][:], in_=z2_banks[t][:])
                 nc.vector.tensor_tensor(out=val["prod", u][:], in0=z1_banks[t][:, cols], in1=z2_copies[t][:, cols], op=ALU.mult)
-                if u == PER_TILE - 1:
-                    quantize(dy_codes, dy_plane, slice(0, N), dy_packed)
+                if u < POOL_SQUARES:
+                    nc.gpsimd.tensor_tensor(out=val["sq", u][:], in0=val["prod", u][:], in1=val["prod", u][:], op=ALU.mult)
                 if u % PER_TILE == PER_TILE - 1:
                     product(z1_banks[t], t, wo, s_o, dy_codes, dy_plane)
-            u = step
-            if 0 <= u < UNITS:
-                nc.scalar.activation(out=val["sq", u][:], in_=val["prod", u][:], func=ACT.Square)
-            u = step - 1
-            if 0 <= u < UNITS:
-                nc.scalar.activation(out=val["inv", u][:], in_=val["root", u][:], func=ACT.Square)
-            u = step
-            if 0 <= u < UNITS:
-                nc.scalar.activation(out=val["root", u][:], in_=val["sq", u][:], func=ACT.Abs_reciprocal_sqrt, bias=place(u)[2])
             u = step - 1
             if 0 <= u < UNITS:
                 t, cols, softener = place(u)
                 nc.vector.scalar_tensor_tensor(
                     out=val["left", u][:], in0=z1_banks[t][:, cols], scalar=softener, in1=val["root", u][:], op0=ALU.mult, op1=ALU.mult
                 )
+                nc.scalar.activation(out=val["inv", u][:], in_=val["root", u][:], func=ACT.Square)
                 nc.vector.tensor_tensor(out=val["right", u][:], in0=z2_banks[t][:, cols], in1=val["inv", u][:], op=ALU.mult)
-            u = step - 2
+                if u < UNITS - 1:
+                    nc.gpsimd.tensor_tensor(out=val["grad", u][:], in0=val["left", u][:], in1=val["right", u][:], op=ALU.mult)
+            u = step
             if 0 <= u < UNITS:
-                engine = nc.gpsimd if u < UNITS - 1 else nc.vector
-                engine.tensor_tensor(out=val["grad", u][:], in0=val["left", u][:], in1=val["right", u][:], op=ALU.mult)
+                nc.scalar.activation(out=val["root", u][:], in_=val["sq", u][:], func=ACT.Abs_reciprocal_sqrt, bias=place(u)[2])
+            u = step + 1
+            if POOL_SQUARES <= u < UNITS:
+                nc.scalar.activation(out=val["sq", u][:], in_=val["prod", u][:], func=ACT.Square)
+            u = step - 2
+            if u == UNITS - 1:
+                nc.vector.tensor_tensor(out=val["grad", u][:], in0=val["left", u][:], in1=val["right", u][:], op=ALU.mult)
             u = step - 3
             if 0 <= u < UNITS:
                 t, cols = place(u)[:2]
                 g, h = TILES[t]
-                engine = nc.gpsimd if u < POOL_SUMS else nc.vector
-                engine.tensor_tensor(out=results[t][:, cols], in0=val["grad", u][:], in1=olds[t][:, cols], op=ALU.add)
+                nc.vector.tensor_tensor(out=results[t][:, cols], in0=val["grad", u][:], in1=olds[t][:, cols], op=ALU.add)
                 if t == len(TILES) - 1:
                     nc.sync.dma_start(out=out[g, P * h : P * (h + 1), cols], in_=results[t][:, cols])
                 elif u % PER_TILE == PER_TILE - 1:

@@ -19,7 +19,7 @@ P = 128
 PACK = 4
 ROWS = D // PACK
 HALVES = M // P
-TILES = [(g, h) for h in range(HALVES) for g in range(G)]
+TILES = [(g, h) for g in range(G) for h in range(HALVES)]
 UNIT = 256
 PER_TILE = N // UNIT
 UNITS = len(TILES) * PER_TILE
@@ -45,10 +45,11 @@ def tile_rows_bagree_kernel(tc, x, w1_words, w1_scales, w2_words, w2_scales, so,
         def load_words(queue, tile, words):
             queue.dma_start(out=tile[:].bitcast(I32), in_=words.rearrange("g p b -> (g p) b").bitcast(I32))
 
-        def load_scales(queue, tile, scales):
-            rows = scales.rearrange("g t m -> (g t) m").bitcast(I32)
-            for q in range(4):
-                queue.dma_start(out=tile[32 * q : 32 * q + 4, :].bitcast(I32), in_=rows[4 * q : 4 * q + 4, :])
+        def load_scales(tile, scales, g):
+            rows = scales[g].bitcast(I32)
+            for q in range(2):
+                first = ROWS * g + 32 * q
+                nc.sync.dma_start(out=tile[first : first + 4, :].bitcast(I32), in_=rows[4 * q : 4 * q + 4, :])
 
         def interleave(copy, packed, raw, cols):
             copy(
@@ -78,7 +79,7 @@ def tile_rows_bagree_kernel(tc, x, w1_words, w1_scales, w2_words, w2_scales, so,
         s1, s2, s_o = plane_tile("s1", M), plane_tile("s2", M), plane_tile("s_o", M)
         x_raw = sb.tile([P, PACK, N], F32, name="x_raw")
         dy_raw = sb.tile([P, PACK, N], F32, name="dy_raw")
-        soft = sb.tile([P, G * HALVES, 8], F32, name="soft")
+        softeners = [sb.tile([P, 1], F32, name="softener%d" % t) for t in range(len(TILES))]
         olds = [sb.tile([P, N], F32, name="old%d" % t) for t in range(len(TILES))]
         results = [sb.tile([P, N], F32, name="result%d" % t) for t in range(len(TILES))]
 
@@ -90,15 +91,18 @@ def tile_rows_bagree_kernel(tc, x, w1_words, w1_scales, w2_words, w2_scales, so,
         nc.sync.dma_start(out=x_raw[:], in_=x.rearrange("g (p j) n -> (g p) j n", j=PACK))
         load_words(nc.sync, w2, w2_words)
         load_words(nc.sync, w1, w1_words)
-        load_scales(nc.sync, s2, w2_scales)
+        load_scales(s2, w2_scales, 0)
+        load_scales(s1, w1_scales, 0)
         nc.sync.dma_start(out=dy_raw[:], in_=dy.rearrange("g (p j) n -> (g p) j n", j=PACK))
         nc.scalar.activation(out=warm[:, 8:9], in_=warm[:, 0:1], func=ACT.Abs_reciprocal_sqrt)
-        load_scales(nc.gpsimd, s1, w1_scales)
+        load_scales(s2, w2_scales, 1)
+        load_scales(s1, w1_scales, 1)
         load_words(nc.sync, wo, wo_words)
-        load_scales(nc.sync, s_o, wo_scales)
-        with nc.allow_non_contiguous_dma(reason="one softener a partition"):
-            nc.sync.dma_start(out=soft[:, :, 0:1], in_=so.rearrange("g (h p) o -> p (g h) o", p=P))
         for t, (g, h) in enumerate(TILES):
+            if h == 0:
+                load_scales(s_o, wo_scales, g)
+            with nc.allow_non_contiguous_dma(reason="one softener a partition"):
+                nc.sync.dma_start(out=softeners[t][:], in_=so[g, P * h : P * (h + 1), :])
             nc.sync.dma_start(out=olds[t][:], in_=old[g, P * h : P * (h + 1), :])
 
         half = N // 2
@@ -114,11 +118,11 @@ def tile_rows_bagree_kernel(tc, x, w1_words, w1_scales, w2_words, w2_scales, so,
 
         z2_banks = [ps.tile([P, N], F32, name="z2_%d" % t) for t in range(len(TILES))]
         z1_banks = [ps.tile([P, N], F32, name="z1_%d" % t) for t in range(len(TILES))]
-        for h in range(HALVES):
-            for t in range(G * h, G * (h + 1)):
-                product(z2_banks[t], t, w2, s2, x_codes, x_plane)
-            for t in range(G * h, G * (h + 1)):
-                product(z1_banks[t], t, w1, s1, x_codes, x_plane)
+        last = len(TILES) - 1
+        product(z2_banks[0], 0, w2, s2, x_codes, x_plane)
+        for t in range(last):
+            product(z2_banks[t + 1], t + 1, w2, s2, x_codes, x_plane)
+            product(z1_banks[t], t, w1, s1, x_codes, x_plane)
 
         dy_packed = sb.tile([P, N, PACK], BF16, name="dy_packed", align_bytes=64)
         dy_codes = sb.tile([P, N], U32, name="dy_codes", align_bytes=64)
@@ -132,9 +136,7 @@ def tile_rows_bagree_kernel(tc, x, w1_words, w1_scales, w2_words, w2_scales, so,
 
         def place(u):
             t = u // PER_TILE
-            g, h = TILES[t]
-            c = HALVES * g + h
-            return t, slice(UNIT * (u % PER_TILE), UNIT * (u % PER_TILE + 1)), soft[:, c, 0:1]
+            return t, slice(UNIT * (u % PER_TILE), UNIT * (u % PER_TILE + 1)), softeners[t][:]
 
         for t in range(len(TILES)):
             nc.scalar.copy(out=z2_copies[t][:], in_=z2_banks[t][:])
@@ -150,6 +152,8 @@ def tile_rows_bagree_kernel(tc, x, w1_words, w1_scales, w2_words, w2_scales, so,
                     nc.gpsimd.tensor_tensor(out=val["sq", u][:], in0=val["prod", u][:], in1=val["prod", u][:], op=ALU.mult)
                 if u % PER_TILE == PER_TILE - 1:
                     product(z1_banks[t], t, wo, s_o, dy_codes, dy_plane)
+                    if t == 0:
+                        product(z1_banks[last], last, w1, s1, x_codes, x_plane)
             u = step - 1
             if 0 <= u < UNITS:
                 t, cols, softener = place(u)

@@ -23,8 +23,7 @@ TILES = [(g, h) for g in range(G) for h in range(HALVES)]
 UNIT = 256
 PER_TILE = N // UNIT
 UNITS = len(TILES) * PER_TILE
-X_VECTOR_COLS = 320
-DY_VECTOR_COLS = 416
+SCALAR_COLS = 128
 POOL_SQUARES = 2
 LEAD = 4
 
@@ -51,11 +50,35 @@ def tile_rows_bagree_kernel(tc, x, w1_words, w1_scales, w2_words, w2_scales, so,
                 first = ROWS * g + 32 * q
                 nc.sync.dma_start(out=tile[first : first + 4, :].bitcast(I32), in_=rows[4 * q : 4 * q + 4, :])
 
-        def interleave(copy, packed, raw, cols):
-            copy(
-                out=packed.rearrange("p (c i) j -> p c j i", i=4),
-                in_=raw[:, :, cols].rearrange("p j (c i) -> p c j i", i=4),
-            )
+        def load_pairs(name, values):
+            rows = values.rearrange("g (p j) n -> (g p) j n", j=PACK)
+            pairs = [sb.tile([P, 2, N], F32, name="%s_pair%d" % (name, a)) for a in range(2)]
+            for a in range(2):
+                nc.sync.dma_start(out=pairs[a][:], in_=rows[:, 2 * a : 2 * a + 2, :])
+            return pairs
+
+        half = N // 2
+        split = N - SCALAR_COLS
+
+        def operand_tiles(name):
+            low = sb.tile([P, half, PACK], BF16, name=name + "_low", align_bytes=64)
+            high = sb.tile([P, half, PACK], BF16, name=name + "_high", align_bytes=64)
+            codes = sb.tile([P, N], U32, name=name + "_codes", align_bytes=64)
+            return low, high, codes, plane_tile(name + "_plane", N)
+
+        def source(pair, lo, hi):
+            return pair[:, :, lo:hi].rearrange("p j n -> p n j")
+
+        def pack_first_pair(pairs, low, high):
+            nc.vector.tensor_copy(out=high[:, :, 0:2], in_=source(pairs[0], half, N))
+            nc.vector.tensor_copy(out=low[:, :, 0:2], in_=source(pairs[0], 0, half))
+
+        def pack_second_pair_on_vector(pairs, low, high):
+            nc.vector.tensor_copy(out=low[:, :, 2:4], in_=source(pairs[1], 0, half))
+            nc.vector.tensor_copy(out=high[:, : split - half, 2:4], in_=source(pairs[1], half, split))
+
+        def pack_second_pair_on_scalar(pairs, high):
+            nc.scalar.copy(out=high[:, split - half :, 2:4], in_=source(pairs[1], split, N))
 
         def quantize(codes, plane, cols, packed):
             nc.vector.quantize_mx(
@@ -77,8 +100,6 @@ def tile_rows_bagree_kernel(tc, x, w1_words, w1_scales, w2_words, w2_scales, so,
 
         w1, w2, wo = words_tile("w1"), words_tile("w2"), words_tile("wo")
         s1, s2, s_o = plane_tile("s1", M), plane_tile("s2", M), plane_tile("s_o", M)
-        x_raw = sb.tile([P, PACK, N], F32, name="x_raw")
-        dy_raw = sb.tile([P, PACK, N], F32, name="dy_raw")
         softeners = [sb.tile([P, 1], F32, name="softener%d" % t) for t in range(len(TILES))]
         olds = [sb.tile([P, N], F32, name="old%d" % t) for t in range(len(TILES))]
         results = [sb.tile([P, N], F32, name="result%d" % t) for t in range(len(TILES))]
@@ -88,12 +109,12 @@ def tile_rows_bagree_kernel(tc, x, w1_words, w1_scales, w2_words, w2_scales, so,
         warm = sb.tile([P, 16], F32, name="warm")
         nc.vector.memset(warm[:, 0:1], 1.0)
         nc.vector.memset(s_o[:].bitcast(I32), 0)
-        nc.sync.dma_start(out=x_raw[:], in_=x.rearrange("g (p j) n -> (g p) j n", j=PACK))
+        x_pairs = load_pairs("x", x)
         load_words(nc.sync, w2, w2_words)
         load_words(nc.sync, w1, w1_words)
         load_scales(s2, w2_scales, 0)
         load_scales(s1, w1_scales, 0)
-        nc.sync.dma_start(out=dy_raw[:], in_=dy.rearrange("g (p j) n -> (g p) j n", j=PACK))
+        dy_pairs = load_pairs("dy", dy)
         nc.scalar.activation(out=warm[:, 8:9], in_=warm[:, 0:1], func=ACT.Abs_reciprocal_sqrt)
         load_scales(s2, w2_scales, 1)
         load_scales(s1, w1_scales, 1)
@@ -105,30 +126,26 @@ def tile_rows_bagree_kernel(tc, x, w1_words, w1_scales, w2_words, w2_scales, so,
                 nc.sync.dma_start(out=softeners[t][:], in_=so[g, P * h : P * (h + 1), :])
             nc.sync.dma_start(out=olds[t][:], in_=old[g, P * h : P * (h + 1), :])
 
-        half = N // 2
-        x_lo = sb.tile([P, half, PACK], BF16, name="x_lo", align_bytes=64)
-        x_hi = sb.tile([P, half, PACK], BF16, name="x_hi", align_bytes=64)
-        x_codes = sb.tile([P, N], U32, name="x_codes", align_bytes=64)
-        x_plane = plane_tile("x_plane", N)
-        interleave(nc.scalar.copy, x_hi[:, X_VECTOR_COLS - half :, :], x_raw, slice(X_VECTOR_COLS, N))
-        interleave(nc.vector.tensor_copy, x_lo[:], x_raw, slice(0, half))
-        interleave(nc.vector.tensor_copy, x_hi[:, : X_VECTOR_COLS - half, :], x_raw, slice(half, X_VECTOR_COLS))
-        quantize(x_codes, x_plane, slice(0, half), x_lo)
-        quantize(x_codes, x_plane, slice(half, N), x_hi)
+        x_low, x_high, x_codes, x_plane = operand_tiles("x")
+        pack_first_pair(x_pairs, x_low, x_high)
+        pack_second_pair_on_scalar(x_pairs, x_high)
+        pack_second_pair_on_vector(x_pairs, x_low, x_high)
+        quantize(x_codes, x_plane, slice(0, half), x_low)
+        quantize(x_codes, x_plane, slice(half, N), x_high)
 
         z2_banks = [ps.tile([P, N], F32, name="z2_%d" % t) for t in range(len(TILES))]
         z1_banks = [ps.tile([P, N], F32, name="z1_%d" % t) for t in range(len(TILES))]
         last = len(TILES) - 1
         product(z2_banks[0], 0, w2, s2, x_codes, x_plane)
-        for t in range(last):
+        product(z1_banks[0], 0, w1, s1, x_codes, x_plane)
+        product(z2_banks[1], 1, w2, s2, x_codes, x_plane)
+        for t in range(1, last):
             product(z2_banks[t + 1], t + 1, w2, s2, x_codes, x_plane)
             product(z1_banks[t], t, w1, s1, x_codes, x_plane)
 
-        dy_packed = sb.tile([P, N, PACK], BF16, name="dy_packed", align_bytes=64)
-        dy_codes = sb.tile([P, N], U32, name="dy_codes", align_bytes=64)
-        dy_plane = plane_tile("dy_plane", N)
-        interleave(nc.scalar.copy, dy_packed[:, DY_VECTOR_COLS:, :], dy_raw, slice(DY_VECTOR_COLS, N))
-        interleave(nc.vector.tensor_copy, dy_packed[:, :DY_VECTOR_COLS, :], dy_raw, slice(0, DY_VECTOR_COLS))
+        dy_low, dy_high, dy_codes, dy_plane = operand_tiles("dy")
+        pack_first_pair(dy_pairs, dy_low, dy_high)
+        pack_second_pair_on_vector(dy_pairs, dy_low, dy_high)
 
         z2_copies = [sb.tile([P, N], F32, name="z2_copy%d" % t) for t in range(len(TILES))]
         stages = ("prod", "sq", "root", "inv", "left", "right", "grad")
@@ -140,11 +157,14 @@ def tile_rows_bagree_kernel(tc, x, w1_words, w1_scales, w2_words, w2_scales, so,
 
         for t in range(len(TILES)):
             nc.scalar.copy(out=z2_copies[t][:], in_=z2_banks[t][:])
+            if t == 0:
+                pack_second_pair_on_scalar(dy_pairs, dy_high)
 
         for step in range(-LEAD, UNITS + 3):
             u = step + LEAD
             if u == 1:
-                quantize(dy_codes, dy_plane, slice(0, N), dy_packed)
+                quantize(dy_codes, dy_plane, slice(0, half), dy_low)
+                quantize(dy_codes, dy_plane, slice(half, N), dy_high)
             if u < UNITS:
                 t, cols = place(u)[:2]
                 nc.vector.tensor_tensor(out=val["prod", u][:], in0=z1_banks[t][:, cols], in1=z2_copies[t][:, cols], op=ALU.mult)

from contextlib import ExitStack

import concourse.mybir as mybir

G, D, M, N = 2, 256, 256, 512
FLOPS = 3 * 2 * G * D * M * N

F32 = mybir.dt.float32
BF16 = mybir.dt.bfloat16
I32 = mybir.dt.int32
U32 = mybir.dt.uint32
U8 = mybir.dt.uint8
FP8X4 = mybir.dt.float8_e4m3fn_x4
FP4X4 = mybir.dt.float4_e2m1fn_x4
ACT = mybir.ActivationFunctionType
ALU = mybir.AluOpType

P = 128
PACK = 4
ROWS = D // PACK
HALVES = M // P
TILES = [(g, h) for g in range(G) for h in range(HALVES)]
UNIT = 256
PER_TILE = N // UNIT
UNITS = len(TILES) * PER_TILE
SCALAR_COLS = 128
POOL_SQUARES = 2
LEAD = 4


def tile_rows_bagree_kernel(tc, x, w1_words, w1_scales, w2_words, w2_scales, so, wo_words, wo_scales, dy, old, out):
    nc = tc.nc
    with ExitStack() as ctx:
        sb = ctx.enter_context(tc.tile_pool(name="sb", bufs=1))
        ps = ctx.enter_context(tc.psum_pool(name="ps", bufs=1))
        ctx.enter_context(tc.manual_schedule())

        def words_tile(name):
            return sb.tile([P, 2 * M], U8, name=name, align_bytes=64)

        def plane_tile(name, width):
            return sb.tile([P, width], U8, name=name, align_bytes=64)

        def load_words(queue, tile, words):
            queue.dma_start(out=tile[:].bitcast(I32), in_=words.rearrange("g p b -> (g p) b").bitcast(I32))

        def load_scales(tile, scales, g):
            rows = scales[g].bitcast(I32)
            for q in range(2):
                first = ROWS * g + 32 * q
                nc.sync.dma_start(out=tile[first : first + 4, :].bitcast(I32), in_=rows[4 * q : 4 * q + 4, :])

        def load_pairs(name, values):
            rows = values.rearrange("g (p j) n -> (g p) j n", j=PACK)
            pairs = [sb.tile([P, 2, N], F32, name="%s_pair%d" % (name, a)) for a in range(2)]
            for a in range(2):
                nc.sync.dma_start(out=pairs[a][:], in_=rows[:, 2 * a : 2 * a + 2, :])
            return pairs

        half = N // 2
        split = N - SCALAR_COLS

        def operand_tiles(name):
            low = sb.tile([P, half, PACK], BF16, name=name + "_low", align_bytes=64)
            high = sb.tile([P, half, PACK], BF16, name=name + "_high", align_bytes=64)
            codes = sb.tile([P, N], U32, name=name + "_codes", align_bytes=64)
            return low, high, codes, plane_tile(name + "_plane", N)

        def source(pair, lo, hi):
            return pair[:, :, lo:hi].rearrange("p j n -> p n j")

        def pack_first_pair(pairs, low, high):
            nc.vector.tensor_copy(out=high[:, :, 0:2], in_=source(pairs[0], half, N))
            nc.vector.tensor_copy(out=low[:, :, 0:2], in_=source(pairs[0], 0, half))

        def pack_second_pair_on_vector(pairs, low, high):
            nc.vector.tensor_copy(out=low[:, :, 2:4], in_=source(pairs[1], 0, half))
            nc.vector.tensor_copy(out=high[:, : split - half, 2:4], in_=source(pairs[1], half, split))

        def pack_second_pair_on_scalar(pairs, high):
            nc.scalar.copy(out=high[:, split - half :, 2:4], in_=source(pairs[1], split, N))

        def quantize(codes, plane, cols, packed):
            nc.vector.quantize_mx(
                out=codes[:, cols].bitcast(FP8X4), scales=plane[:, cols], in_=packed[:].rearrange("p n j -> p (n j)")
            )

        def product(bank, t, words, w_plane, codes, plane):
            g, h = TILES[t]
            rows = slice(ROWS * g, ROWS * (g + 1))
            nc.tensor.matmul_mx(
                out=bank[:],
                lhsT=words[rows, 2 * P * h : 2 * P * (h + 1)].bitcast(FP4X4),
                lhsT_scale=w_plane[rows, P * h : P * (h + 1)],
                rhs=codes[rows, :].bitcast(FP8X4),
                rhs_scale=plane[rows, :],
                start=True,
                stop=True,
            )

        w1, w2, wo = words_tile("w1"), words_tile("w2"), words_tile("wo")
        s1, s2, s_o = plane_tile("s1", M), plane_tile("s2", M), plane_tile("s_o", M)
        softeners = [sb.tile([P, 1], F32, name="softener%d" % t) for t in range(len(TILES))]
        olds = [sb.tile([P, N], F32, name="old%d" % t) for t in range(len(TILES))]
        results = [sb.tile([P, N], F32, name="result%d" % t) for t in range(len(TILES))]

        nc.vector.memset(s2[:].bitcast(I32), 0)
        nc.gpsimd.memset(s1[:].bitcast(I32), 0)
        warm = sb.tile([P, 16], F32, name="warm")
        nc.vector.memset(warm[:, 0:1], 1.0)
        nc.vector.memset(s_o[:].bitcast(I32), 0)
        x_pairs = load_pairs("x", x)
        load_words(nc.sync, w2, w2_words)
        load_words(nc.sync, w1, w1_words)
        load_scales(s2, w2_scales, 0)
        load_scales(s1, w1_scales, 0)
        dy_pairs = load_pairs("dy", dy)
        nc.scalar.activation(out=warm[:, 8:9], in_=warm[:, 0:1], func=ACT.Abs_reciprocal_sqrt)
        load_scales(s2, w2_scales, 1)
        load_scales(s1, w1_scales, 1)
        load_words(nc.sync, wo, wo_words)
        for t, (g, h) in enumerate(TILES):
            if h == 0:
                load_scales(s_o, wo_scales, g)
            with nc.allow_non_contiguous_dma(reason="one softener a partition"):
                nc.sync.dma_start(out=softeners[t][:], in_=so[g, P * h : P * (h + 1), :])
            nc.sync.dma_start(out=olds[t][:], in_=old[g, P * h : P * (h + 1), :])

        x_low, x_high, x_codes, x_plane = operand_tiles("x")
        pack_first_pair(x_pairs, x_low, x_high)
        pack_second_pair_on_scalar(x_pairs, x_high)
        pack_second_pair_on_vector(x_pairs, x_low, x_high)
        quantize(x_codes, x_plane, slice(0, half), x_low)
        quantize(x_codes, x_plane, slice(half, N), x_high)

        z2_banks = [ps.tile([P, N], F32, name="z2_%d" % t) for t in range(len(TILES))]
        z1_banks = [ps.tile([P, N], F32, name="z1_%d" % t) for t in range(len(TILES))]
        last = len(TILES) - 1
        product(z2_banks[0], 0, w2, s2, x_codes, x_plane)
        product(z1_banks[0], 0, w1, s1, x_codes, x_plane)
        product(z2_banks[1], 1, w2, s2, x_codes, x_plane)
        for t in range(1, last):
            product(z2_banks[t + 1], t + 1, w2, s2, x_codes, x_plane)
            product(z1_banks[t], t, w1, s1, x_codes, x_plane)

        dy_low, dy_high, dy_codes, dy_plane = operand_tiles("dy")
        pack_first_pair(dy_pairs, dy_low, dy_high)
        pack_second_pair_on_vector(dy_pairs, dy_low, dy_high)

        z2_copies = [sb.tile([P, N], F32, name="z2_copy%d" % t) for t in range(len(TILES))]
        stages = ("prod", "sq", "root", "inv", "left", "right", "grad")
        val = {(k, u): sb.tile([P, UNIT], F32, name="%s%d" % (k, u)) for k in stages for u in range(UNITS)}

        def place(u):
            t = u // PER_TILE
            return t, slice(UNIT * (u % PER_TILE), UNIT * (u % PER_TILE + 1)), softeners[t][:]

        for t in range(len(TILES)):
            nc.scalar.copy(out=z2_copies[t][:], in_=z2_banks[t][:])
            if t == 0:
                pack_second_pair_on_scalar(dy_pairs, dy_high)

        for step in range(-LEAD, UNITS + 3):
            u = step + LEAD
            if u == 1:
                quantize(dy_codes, dy_plane, slice(0, half), dy_low)
                quantize(dy_codes, dy_plane, slice(half, N), dy_high)
            if u < UNITS:
                t, cols = place(u)[:2]
                nc.vector.tensor_tensor(out=val["prod", u][:], in0=z1_banks[t][:, cols], in1=z2_copies[t][:, cols], op=ALU.mult)
                if u < POOL_SQUARES:
                    nc.gpsimd.tensor_tensor(out=val["sq", u][:], in0=val["prod", u][:], in1=val["prod", u][:], op=ALU.mult)
                if u % PER_TILE == PER_TILE - 1:
                    product(z1_banks[t], t, wo, s_o, dy_codes, dy_plane)
                    if t == 0:
                        product(z1_banks[last], last, w1, s1, x_codes, x_plane)
            u = step - 1
            if 0 <= u < UNITS:
                t, cols, softener = place(u)
                nc.vector.scalar_tensor_tensor(
                    out=val["left", u][:], in0=z1_banks[t][:, cols], scalar=softener, in1=val["root", u][:], op0=ALU.mult, op1=ALU.mult
                )
                nc.scalar.activation(out=val["inv", u][:], in_=val["root", u][:], func=ACT.Square)
                nc.vector.tensor_tensor(out=val["right", u][:], in0=z2_banks[t][:, cols], in1=val["inv", u][:], op=ALU.mult)
                if u < UNITS - 1:
                    nc.gpsimd.tensor_tensor(out=val["grad", u][:], in0=val["left", u][:], in1=val["right", u][:], op=ALU.mult)
            u = step
            if 0 <= u < UNITS:
                nc.scalar.activation(out=val["root", u][:], in_=val["sq", u][:], func=ACT.Abs_reciprocal_sqrt, bias=place(u)[2])
            u = step + 1
            if POOL_SQUARES <= u < UNITS:
                nc.scalar.activation(out=val["sq", u][:], in_=val["prod", u][:], func=ACT.Square)
            u = step - 2
            if u == UNITS - 1:
                nc.vector.tensor_tensor(out=val["grad", u][:], in0=val["left", u][:], in1=val["right", u][:], op=ALU.mult)
            u = step - 3
            if 0 <= u < UNITS:
                t, cols = place(u)[:2]
                g, h = TILES[t]
                nc.vector.tensor_tensor(out=results[t][:, cols], in0=val["grad", u][:], in1=olds[t][:, cols], op=ALU.add)
                if t == len(TILES) - 1:
                    nc.sync.dma_start(out=out[g, P * h : P * (h + 1), cols], in_=results[t][:, cols])
                elif u % PER_TILE == PER_TILE - 1:
                    nc.sync.dma_start(out=out[g, P * h : P * (h + 1), :], in_=results[t][:])
